import numpy as np
import ml_dtypes


def mxq(x, axis, fmt="e4m3"):
    dtype, down = {"e4m3": (ml_dtypes.float8_e4m3fn, 7), "e5m2": (ml_dtypes.float8_e5m2, 14)}[fmt]
    v = np.moveaxis(np.asarray(x, np.float32).astype(ml_dtypes.bfloat16).astype(np.float64), axis, -1)
    blocks = v.reshape(v.shape[:-1] + (-1, 32))
    amax = np.abs(blocks).max(-1, keepdims=True)
    byte = np.maximum(np.where(amax > 0, np.frexp(amax)[1] - 1 + 127, 0) - down, 1)
    scale = np.exp2(byte - 127.0)
    codes = (blocks / scale).astype(np.float32).astype(dtype).astype(np.float64)
    return np.moveaxis((codes * scale).reshape(v.shape), -1, axis)


WIDE = False


def mx_kscale(k):
    if not WIDE:
        return np.ones(k)
    levels = np.array([10, -10, 5, -5, 0])
    if k % 512:
        return np.exp2(np.random.permutation(np.resize(levels, k // 32))).repeat(32)
    a = np.empty((k // 512, 16))
    for p in range(k // 512):
        a[p, :8] = np.random.permutation(np.resize(levels, 8))
        for g in range(8):
            far = levels[np.abs(levels - a[p, g]) >= 10]
            a[p, g + 8] = far[np.random.randint(len(far))]
    return np.exp2(a.ravel()).repeat(32)


def f64(x):
    return np.asarray(x).astype(np.float64)


def striped8(idx):
    return np.asarray(idx).reshape(8, -1, 16).transpose(0, 2, 1).reshape(128, -1).astype(np.uint16)


def unstriped8(offs):
    return offs.reshape(8, 16, -1).transpose(0, 2, 1).reshape(8, -1).astype(np.int64)


def pick8(x, idx, run):
    r = np.arange(len(x))
    return x[r[:, None], idx[r % (8 * run) // run]]


E2M1 = np.array([0.0, 0.5, 1.0, 1.5, 2.0, 3.0, 4.0, 6.0, -0.0, -0.5, -1.0, -1.5, -2.0, -3.0, -4.0, -6.0])


def pack_weight(w, fmt):
    k, n = w.shape
    w = f64(np.asarray(w, np.float32).astype(ml_dtypes.bfloat16)).reshape(k // 32, 32, n)
    amax = np.abs(w).max(1)
    if fmt == "e4m3":
        byte = np.frexp(amax)[1] - 1 + 127 - 7
    else:
        mant, ex = np.frexp(amax / 6.0)
        byte = np.where(mant > 0.5, ex, ex - 1) + 127
    byte = np.clip(np.where(amax > 0, byte, 1), 1, 254)
    scaled = (w * np.exp2(127.0 - byte)[:, None, :]).reshape(k, n).astype(np.float32)
    by_word = np.ascontiguousarray(scaled.reshape(k // 512, 128, 4, n).transpose(0, 1, 3, 2))
    if fmt == "e4m3":
        words = by_word.astype(ml_dtypes.float8_e4m3fn).view(np.uint8)
    else:
        c = by_word.astype(ml_dtypes.float4_e2m1fn).view(np.uint8) & 0xF
        words = (c[..., 0::2] | (c[..., 1::2] << 4)).reshape(k // 512, 128, 2 * n)
    return np.ascontiguousarray(words), np.ascontiguousarray(byte.astype(np.uint8).reshape(k // 512, 16, n))


def unpack_weight(words, scales, fmt):
    g, _, n = scales.shape
    words = np.ascontiguousarray(words).reshape(g, 128, n, -1)
    if fmt == "e4m3":
        vals = words.view(ml_dtypes.float8_e4m3fn).astype(np.float64)
    else:
        nib = np.empty((g, 128, n, 4), np.uint8)
        nib[..., 0::2] = words & 0xF
        nib[..., 1::2] = words >> 4
        vals = E2M1[nib]
    vals = vals * np.repeat(np.exp2(scales.astype(np.float64) - 127.0), 8, axis=1)[..., None]
    return vals.transpose(0, 1, 3, 2).reshape(g * 512, n)


def sigmoid(v):
    return 1.0 / (1.0 + np.exp(-v))


D, T, U, Z, I, Q, E = 512, 1024, 1024, 1024, 512, 512, 256


def setup_inputs():
    n = np.random.standard_normal
    idx = np.stack([np.random.permutation(T)[:I] for _ in range(8)])
    idx2 = np.stack([np.random.permutation(U)[:I] for _ in range(8)])
    idx3 = np.stack([np.random.permutation(Z)[:I] for _ in range(8)])
    idx4 = np.stack([np.random.permutation(Z)[:I] for _ in range(8)])
    fd = mx_kscale(D)
    fq = mx_kscale(Q)
    keysp = pack_weight(n((D, T)) / fd[:, None], "e2m1")
    notesp = pack_weight(n((D, U)) / fd[:, None], "e4m3")
    mixp = pack_weight(n((Q, E)) * 1.0 / np.sqrt(Q) / fq[:, None], "e4m3")
    return {
        "query": (n((D, Q)) * 1.0 / np.sqrt(D) * fd[:, None]).astype(np.float32),
        "query2": (n((D, Q)) * 1.0 / np.sqrt(D) * fd[:, None]).astype(np.float32),
        "keys_words": keysp[0],
        "keys_scales": keysp[1],
        "notes_words": notesp[0],
        "notes_scales": notesp[1],
        "thr": (np.random.uniform(-0.6, 0.6, (Q, 1))).astype(np.float32),
        "slope": (np.random.uniform(1.0, 3.0, (Q, 1))).astype(np.float32),
        "rowf": (np.random.uniform(0.5, 2.0, (Q, 1)) * fq[:, None]).astype(np.float32),
        "mix_words": mixp[0],
        "mix_scales": mixp[1],
        "offs": striped8(idx),
        "offs2": striped8(idx2),
        "offs3": striped8(idx3),
        "offs4": striped8(idx4),
    }


def reference(query, query2, keys_words, keys_scales, notes_words, notes_scales, thr, slope, rowf, mix_words, mix_scales, offs, offs2, offs3, offs4):
    idx = unstriped8(offs)
    idx2 = unstriped8(offs2)
    idx3 = unstriped8(offs3)
    idx4 = unstriped8(offs4)
    keysu = unpack_weight(keys_words, keys_scales, "e2m1")
    notesu = unpack_weight(notes_words, notes_scales, "e4m3")
    mixu = unpack_weight(mix_words, mix_scales, "e4m3")
    queryq = mxq(f64(query), 0, "e4m3")
    a = queryq.T @ keysu
    query2q = mxq(f64(query2), 0, "e4m3")
    b = query2q.T @ notesu
    s1 = sigmoid(pick8(a, idx, 64) * f64(slope) + f64(thr))
    w = pick8(b, idx2, 64) * s1
    f1 = np.zeros((Q, Z))
    f1[np.arange(Q)[:, None], idx3[np.arange(Q) % 512 // 64]] = w
    v = pick8(f1, idx4, 64) - s1
    g = v * 2.0 + pick8(b, idx2, 64)
    gw = g * f64(rowf)
    gwq = mxq(gw, 0, "e4m3")
    y = mixu.T @ gwq
    return y

@@ -1,0 +1,201 @@
+from contextlib import ExitStack
+
+import concourse.mybir as mybir
+
+F32 = mybir.dt.float32
+BF16 = mybir.dt.bfloat16
+I32 = mybir.dt.int32
+U32 = mybir.dt.uint32
+U16 = mybir.dt.uint16
+U8 = mybir.dt.uint8
+FP8X4 = mybir.dt.float8_e4m3fn_x4
+FP4X4 = mybir.dt.float4_e2m1fn_x4
+ALU = mybir.AluOpType
+ACT = mybir.ActivationFunctionType
+
+P = 128
+PACK = 4
+D, T, U, Z, SLOTS, Q, E = 512, 1024, 1024, 1024, 512, 512, 256
+BANK = 512
+HALF = 256
+
+FLOPS = 2 * D * Q * T + 2 * D * Q * U + 2 * Q * E * SLOTS
+
+
+def tile_attend_openbridge_twoq_mixed_kernel(
+    tc, query, query2, keys_words, keys_scales, notes_words, notes_scales, thr, slope, rowf,
+    mix_words, mix_scales, offs, offs2, offs3, offs4, out,
+):
+    nc = tc.nc
+    with ExitStack() as ctx:
+        keep = ctx.enter_context(tc.tile_pool(name="keep", bufs=1))
+        psum = ctx.enter_context(tc.psum_pool(name="psum", bufs=8))
+
+        def scale_plane(name, source, width, queue):
+            plane = keep.tile([P, width], U8, name=name, align_bytes=64)
+            nc.vector.memset(plane[:].bitcast(I32), 0)
+            for r in range(4):
+                queue.dma_start(out=plane[r:P:32, :].bitcast(I32), in_=source[0, r:16:4, :].bitcast(I32))
+            return plane
+
+        def load_rows(name, source, half):
+            raw = keep.tile([P, PACK, HALF], F32, name=name)
+            cols = slice(half * HALF, (half + 1) * HALF)
+            nc.sync.dma_start(out=raw[:], in_=source.rearrange("(p j) q -> p j q", j=PACK)[:, :, cols])
+            return raw
+
+        def load_list(name, source):
+            offsets = keep.tile([P, SLOTS // 16], U16, name=name)
+            nc.sync.dma_start(offsets[:], source)
+            return offsets
+
+        def load_vector(name, source, queue):
+            vec = keep.tile([P, PACK], F32, name=name)
+            queue.dma_start(out=vec[:], in_=source.rearrange("(p t) o -> p (t o)", t=PACK))
+            return vec
+
+        def load_words(name, source, cols):
+            words = keep.tile([P, cols.stop - cols.start], U32, name=name, align_bytes=64)
+            nc.sync.dma_start(
+                out=words[:].bitcast(I32), in_=source[0].rearrange("p n t -> p (n t)").bitcast(I32)[:, cols]
+            )
+            return words
+
+        key_scales = scale_plane("key_scales", keys_scales, T, nc.sync)
+        q_raw = [load_rows("q_raw%d" % h, query, h) for h in range(2)]
+        key_words = keep.tile([P, 2 * T], U8, name="key_words", align_bytes=64)
+        nc.sync.dma_start(out=key_words[:].bitcast(I32), in_=keys_words[0].bitcast(I32))
+        a_list = load_list("a_list", offs)
+        slope_t = load_vector("slope_t", slope, nc.gpsimd)
+        thr_t = load_vector("thr_t", thr, nc.gpsimd)
+        note_scales = scale_plane("note_scales", notes_scales, U, nc.scalar)
+        q2_raw = [load_rows("q2_raw%d" % h, query2, h) for h in range(2)]
+        note_words = [load_words("note_words%d" % h, notes_words, slice(h * BANK, (h + 1) * BANK)) for h in range(2)]
+        b_list = load_list("b_list", offs2)
+        put_list = load_list("put_list", offs3)
+        get_list = load_list("get_list", offs4)
+        rowf_t = load_vector("rowf_t", rowf, nc.sync)
+        mix_w = load_words("mix_w", mix_words, slice(0, E))
+        mix_s = scale_plane("mix_s", mix_scales, E, nc.sync)
+
+        places = [keep.tile([P, Z], F32, name="places%d" % t) for t in range(PACK)]
+        for t in range(PACK):
+            nc.vector.memset(places[t][:], 0.0)
+
+        def quantise_queries(name, raw):
+            dealt = keep.tile([P, PACK, P, PACK], BF16, name=name + "_dealt", align_bytes=64)
+            codes = keep.tile([P, Q], U32, name=name + "_codes", align_bytes=64)
+            scales = keep.tile([P, Q], U8, name=name + "_scales", align_bytes=64)
+            for pair in range(2):
+                ts = slice(2 * pair, 2 * pair + 2)
+                for h in range(2):
+                    nc.vector.tensor_copy(
+                        out=dealt[:, ts, h * 64:(h + 1) * 64, :].rearrange("p t m j -> p m j t"),
+                        in_=raw[h][:].rearrange("p j (m t) -> p m j t", t=PACK)[:, :, :, ts],
+                    )
+                for t in range(2 * pair, 2 * pair + 2):
+                    nc.vector.quantize_mx(
+                        out=codes[:, t * P:(t + 1) * P].bitcast(FP8X4),
+                        scales=scales[:, t * P:(t + 1) * P],
+                        in_=dealt[:, t].rearrange("p m j -> p (m j)"),
+                    )
+            return codes, scales
+
+        q_codes, q_scales = quantise_queries("q", q_raw)
+        q2_codes, q2_scales = quantise_queries("q2", q2_raw)
+
+        twice_rowf = keep.tile([P, PACK], F32, name="twice_rowf")
+        nc.vector.tensor_scalar(twice_rowf[:], rowf_t[:], 2.0, None, ALU.mult)
+
+        gw = keep.tile([P, PACK, SLOTS], F32, name="gw")
+
+        def scores(name, t, codes, scales, moving, moving_scales, copy_engines):
+            rows = keep.tile([P, 2 * BANK], F32, name="%s%d" % (name, t))
+            for h in range(2):
+                bank = psum.tile([P, BANK], F32, name="bank")
+                nc.tensor.matmul_mx(
+                    out=bank[:],
+                    lhsT=codes[:, t * P:(t + 1) * P].bitcast(FP8X4),
+                    lhsT_scale=scales[:, t * P:(t + 1) * P],
+                    rhs=moving[h],
+                    rhs_scale=moving_scales[:, h * BANK:(h + 1) * BANK],
+                    start=True,
+                    stop=True,
+                )
+                copy_engines[h](rows[:, h * BANK:(h + 1) * BANK], bank[:])
+            return rows
+
+        keys_moving = [key_words[:, h * 2 * BANK:(h + 1) * 2 * BANK].bitcast(FP4X4) for h in range(2)]
+        notes_moving = [note_words[h][:].bitcast(FP8X4) for h in range(2)]
+        on_scalar = (nc.scalar.copy, nc.scalar.copy)
+        shared = (nc.vector.tensor_copy, nc.scalar.copy)
+
+        gates, notes, rests, found = [], [], [], []
+        for t in range(PACK):
+            a = scores("a", t, q_codes, q_scales, keys_moving, key_scales, on_scalar)
+            gate = keep.tile([P, SLOTS], F32, name="gate%d" % t)
+            nc.scalar.activation(
+                gate[:], a[:].indirect(a_list[:]), ACT.Sigmoid, bias=thr_t[:, t:t + 1], scale=slope_t[:, t:t + 1]
+            )
+            b = scores("b", t, q2_codes, q2_scales, notes_moving, note_scales, shared if t == 0 else on_scalar)
+            note = keep.tile([P, SLOTS], F32, name="note%d" % t)
+            if t == 0:
+                nc.vector.tensor_copy(note[:, :HALF], b[:].indirect(b_list[:, 0:16]))
+                nc.scalar.activation(note[:, HALF:], b[:].indirect(b_list[:, 16:32]), ACT.Copy)
+            else:
+                nc.scalar.activation(note[:], b[:].indirect(b_list[:]), ACT.Copy)
+            nc.vector.tensor_tensor(places[t][:].indirect(put_list[:]), note[:], gate[:], ALU.mult)
+            rest = keep.tile([P, SLOTS], F32, name="rest%d" % t)
+            nc.vector.scalar_tensor_tensor(rest[:], note[:], 0.5, gate[:], ALU.mult, ALU.subtract)
+            gates.append(gate)
+            notes.append(note)
+            rests.append(rest)
+
+        half_g = [keep.tile([P, SLOTS], F32, name="half_g%d" % t) for t in range(PACK)]
+        for t in range(PACK - 1):
+            if t == 0:
+                nc.vector.tensor_tensor(half_g[t][:], places[t][:].indirect(get_list[:]), rests[t][:], ALU.add)
+            else:
+                got = keep.tile([P, SLOTS], F32, name="got%d" % t)
+                nc.scalar.activation(got[:], places[t][:].indirect(get_list[:]), ACT.Copy)
+                nc.vector.tensor_tensor(half_g[t][:], got[:], rests[t][:], ALU.add)
+            nc.scalar.activation(gw[:, t, :], half_g[t][:], ACT.Copy, scale=twice_rowf[:, t:t + 1])
+
+        last = PACK - 1
+        woven = keep.tile([P, SLOTS, PACK], BF16, name="woven", align_bytes=64)
+        gw_codes = keep.tile([P, SLOTS], U32, name="gw_codes", align_bytes=64)
+        gw_scales = keep.tile([P, SLOTS], U8, name="gw_scales", align_bytes=64)
+        got_last = keep.tile([P, HALF], F32, name="got_last")
+        nc.scalar.activation(got_last[:], places[last][:].indirect(get_list[:, 16:32]), ACT.Copy)
+        for h in range(2):
+            cols = slice(h * HALF, (h + 1) * HALF)
+            if h == 0:
+                nc.vector.tensor_tensor(
+                    half_g[last][:, cols], places[last][:].indirect(get_list[:, 0:16]), rests[last][:, cols], ALU.add
+                )
+            else:
+                nc.vector.tensor_tensor(half_g[last][:, cols], got_last[:], rests[last][:, cols], ALU.add)
+            nc.vector.tensor_scalar(gw[:, last, cols], half_g[last][:, cols], twice_rowf[:, last:last + 1], None, ALU.mult)
+            nc.vector.tensor_copy(
+                out=woven[:, cols, :].rearrange("p (c i) t -> p c t i", i=2),
+                in_=gw[:, :, cols].rearrange("p t (c i) -> p c t i", i=2),
+            )
+            nc.vector.quantize_mx(
+                out=gw_codes[:, cols].bitcast(FP8X4),
+                scales=gw_scales[:, cols],
+                in_=woven[:, cols, :].rearrange("p i t -> p (i t)"),
+            )
+            bank = psum.tile([P, BANK], F32, name="bank")
+            for c in range(2):
+                nc.tensor.matmul_mx(
+                    out=bank[:, c * HALF:(c + 1) * HALF],
+                    lhsT=mix_w[:, c * P:(c + 1) * P].bitcast(FP8X4),
+                    lhsT_scale=mix_s[:, c * P:(c + 1) * P],
+                    rhs=gw_codes[:, cols].bitcast(FP8X4),
+                    rhs_scale=gw_scales[:, cols],
+                    start=True,
+                    stop=True,
+                )
+            result = keep.tile([P, 2, HALF], F32, name="result%d" % h)
+            nc.scalar.copy(result[:].rearrange("p c i -> p (c i)"), bank[:])
+            nc.sync.dma_start(out=out.rearrange("(c e) i -> e c i", c=2)[:, :, cols], in_=result[:])

@@ -29,19 +29,17 @@ def tile_attend_openbridge_twoq_mixed_kernel(
     nc = tc.nc
     with ExitStack() as ctx:
         keep = ctx.enter_context(tc.tile_pool(name="keep", bufs=1))
-        psum = ctx.enter_context(tc.psum_pool(name="psum", bufs=8))
+        psum = ctx.enter_context(tc.psum_pool(name="psum", bufs=1))
 
         def scale_plane(name, source, width, queue):
             plane = keep.tile([P, width], U8, name=name, align_bytes=64)
-            nc.vector.memset(plane[:].bitcast(I32), 0)
             for r in range(4):
                 queue.dma_start(out=plane[r:P:32, :].bitcast(I32), in_=source[0, r:16:4, :].bitcast(I32))
             return plane
 
-        def load_rows(name, source, half):
-            raw = keep.tile([P, PACK, HALF], F32, name=name)
-            cols = slice(half * HALF, (half + 1) * HALF)
-            nc.sync.dma_start(out=raw[:], in_=source.rearrange("(p j) q -> p j q", j=PACK)[:, :, cols])
+        def load_rows(name, source):
+            raw = keep.tile([P, PACK, Q], F32, name=name)
+            nc.sync.dma_start(out=raw[:], in_=source.rearrange("(p j) q -> p j q", j=PACK))
             return raw
 
         def load_list(name, source):
@@ -61,58 +59,57 @@ def tile_attend_openbridge_twoq_mixed_kernel(
             )
             return words
 
+        q_raw = load_rows("q_raw", query)
         key_scales = scale_plane("key_scales", keys_scales, T, nc.sync)
-        q_raw = [load_rows("q_raw%d" % h, query, h) for h in range(2)]
         key_words = keep.tile([P, 2 * T], U8, name="key_words", align_bytes=64)
         nc.sync.dma_start(out=key_words[:].bitcast(I32), in_=keys_words[0].bitcast(I32))
         a_list = load_list("a_list", offs)
         slope_t = load_vector("slope_t", slope, nc.gpsimd)
         thr_t = load_vector("thr_t", thr, nc.gpsimd)
-        note_scales = scale_plane("note_scales", notes_scales, U, nc.scalar)
-        q2_raw = [load_rows("q2_raw%d" % h, query2, h) for h in range(2)]
-        note_words = [load_words("note_words%d" % h, notes_words, slice(h * BANK, (h + 1) * BANK)) for h in range(2)]
+        q2_raw = load_rows("q2_raw", query2)
+        note_words = load_words("note_words", notes_words, slice(0, U))
+        note_scales = scale_plane("note_scales", notes_scales, U, nc.sync)
         b_list = load_list("b_list", offs2)
         put_list = load_list("put_list", offs3)
-        get_list = load_list("get_list", offs4)
         rowf_t = load_vector("rowf_t", rowf, nc.sync)
+        get_list = load_list("get_list", offs4)
         mix_w = load_words("mix_w", mix_words, slice(0, E))
         mix_s = scale_plane("mix_s", mix_scales, E, nc.sync)
 
         places = [keep.tile([P, Z], F32, name="places%d" % t) for t in range(PACK)]
-        for t in range(PACK):
-            nc.vector.memset(places[t][:], 0.0)
+        for tile in places:
+            nc.vector.memset(tile[:], 0.0)
 
-        def quantise_queries(name, raw):
-            dealt = keep.tile([P, PACK, P, PACK], BF16, name=name + "_dealt", align_bytes=64)
+        def quantise_queries(name, raw, staging):
             codes = keep.tile([P, Q], U32, name=name + "_codes", align_bytes=64)
             scales = keep.tile([P, Q], U8, name=name + "_scales", align_bytes=64)
             for pair in range(2):
                 ts = slice(2 * pair, 2 * pair + 2)
-                for h in range(2):
-                    nc.vector.tensor_copy(
-                        out=dealt[:, ts, h * 64:(h + 1) * 64, :].rearrange("p t m j -> p m j t"),
-                        in_=raw[h][:].rearrange("p j (m t) -> p m j t", t=PACK)[:, :, :, ts],
-                    )
+                dealt = keep.tile([P, 2, P, PACK], BF16, name=staging[pair], align_bytes=64)
+                nc.vector.tensor_copy(
+                    out=dealt[:].rearrange("p t m j -> p m j t"),
+                    in_=raw[:].rearrange("p j (m t) -> p m j t", t=PACK)[:, :, :, ts],
+                )
                 for t in range(2 * pair, 2 * pair + 2):
                     nc.vector.quantize_mx(
                         out=codes[:, t * P:(t + 1) * P].bitcast(FP8X4),
                         scales=scales[:, t * P:(t + 1) * P],
-                        in_=dealt[:, t].rearrange("p m j -> p (m j)"),
+                        in_=dealt[:, t % 2].rearrange("p m j -> p (m j)"),
                     )
             return codes, scales
 
-        q_codes, q_scales = quantise_queries("q", q_raw)
-        q2_codes, q2_scales = quantise_queries("q2", q2_raw)
+        q_codes, q_scales = quantise_queries("q", q_raw, ("q_dealt", "q_dealt"))
+        q2_codes, q2_scales = quantise_queries("q2", q2_raw, ("q2_dealt0", "q2_dealt1"))
 
         twice_rowf = keep.tile([P, PACK], F32, name="twice_rowf")
         nc.vector.tensor_scalar(twice_rowf[:], rowf_t[:], 2.0, None, ALU.mult)
 
         gw = keep.tile([P, PACK, SLOTS], F32, name="gw")
 
-        def scores(name, t, codes, scales, moving, moving_scales, copy_engines):
+        def scores(name, t, codes, scales, moving, moving_scales, copy_engines, pair):
             rows = keep.tile([P, 2 * BANK], F32, name="%s%d" % (name, t))
             for h in range(2):
-                bank = psum.tile([P, BANK], F32, name="bank")
+                bank = psum.tile([P, BANK], F32, name="bank%d" % (2 * pair + h))
                 nc.tensor.matmul_mx(
                     out=bank[:],
                     lhsT=codes[:, t * P:(t + 1) * P].bitcast(FP8X4),
@@ -126,57 +123,60 @@ def tile_attend_openbridge_twoq_mixed_kernel(
             return rows
 
         keys_moving = [key_words[:, h * 2 * BANK:(h + 1) * 2 * BANK].bitcast(FP4X4) for h in range(2)]
-        notes_moving = [note_words[h][:].bitcast(FP8X4) for h in range(2)]
+        notes_moving = [note_words[:, h * BANK:(h + 1) * BANK].bitcast(FP8X4) for h in range(2)]
         on_scalar = (nc.scalar.copy, nc.scalar.copy)
-        shared = (nc.vector.tensor_copy, nc.scalar.copy)
+        shared = (nc.scalar.copy, nc.vector.tensor_copy)
 
-        gates, notes, rests, found = [], [], [], []
+        on_vector = (nc.vector.tensor_copy, nc.vector.tensor_copy)
+        rests = []
         for t in range(PACK):
-            a = scores("a", t, q_codes, q_scales, keys_moving, key_scales, on_scalar)
+            a = scores("a", t, q_codes, q_scales, keys_moving, key_scales, on_scalar, t)
             gate = keep.tile([P, SLOTS], F32, name="gate%d" % t)
             nc.scalar.activation(
                 gate[:], a[:].indirect(a_list[:]), ACT.Sigmoid, bias=thr_t[:, t:t + 1], scale=slope_t[:, t:t + 1]
             )
-            b = scores("b", t, q2_codes, q2_scales, notes_moving, note_scales, shared if t == 0 else on_scalar)
+            b = scores("b", t, q2_codes, q2_scales, notes_moving, note_scales,
+                       on_vector if t == 0 else on_scalar, (t + 2) % 4)
             note = keep.tile([P, SLOTS], F32, name="note%d" % t)
             if t == 0:
-                nc.vector.tensor_copy(note[:, :HALF], b[:].indirect(b_list[:, 0:16]))
-                nc.scalar.activation(note[:, HALF:], b[:].indirect(b_list[:, 16:32]), ACT.Copy)
+                nc.vector.tensor_copy(note[:], b[:].indirect(b_list[:]))
             else:
                 nc.scalar.activation(note[:], b[:].indirect(b_list[:]), ACT.Copy)
             nc.vector.tensor_tensor(places[t][:].indirect(put_list[:]), note[:], gate[:], ALU.mult)
+            scaled_gate = keep.tile([P, SLOTS], F32, name="scaled_gate%d" % t)
+            if t < 2:
+                nc.vector.tensor_scalar(scaled_gate[:], gate[:], twice_rowf[:, t:t + 1], None, ALU.mult)
+            else:
+                nc.scalar.activation(scaled_gate[:], gate[:], ACT.Copy, scale=twice_rowf[:, t:t + 1])
             rest = keep.tile([P, SLOTS], F32, name="rest%d" % t)
-            nc.vector.scalar_tensor_tensor(rest[:], note[:], 0.5, gate[:], ALU.mult, ALU.subtract)
-            gates.append(gate)
-            notes.append(note)
+            nc.vector.scalar_tensor_tensor(
+                rest[:], note[:], rowf_t[:, t:t + 1], scaled_gate[:], ALU.mult, ALU.subtract
+            )
             rests.append(rest)
 
-        half_g = [keep.tile([P, SLOTS], F32, name="half_g%d" % t) for t in range(PACK)]
-        for t in range(PACK - 1):
-            if t == 0:
-                nc.vector.tensor_tensor(half_g[t][:], places[t][:].indirect(get_list[:]), rests[t][:], ALU.add)
-            else:
-                got = keep.tile([P, SLOTS], F32, name="got%d" % t)
-                nc.scalar.activation(got[:], places[t][:].indirect(get_list[:]), ACT.Copy)
-                nc.vector.tensor_tensor(half_g[t][:], got[:], rests[t][:], ALU.add)
-            nc.scalar.activation(gw[:, t, :], half_g[t][:], ACT.Copy, scale=twice_rowf[:, t:t + 1])
-
         last = PACK - 1
+        got = [keep.tile([P, SLOTS], F32, name="got%d" % t) for t in range(PACK)]
+        for t in range(last):
+            nc.scalar.activation(got[t][:], places[t][:].indirect(get_list[:]), ACT.Copy)
+            nc.vector.scalar_tensor_tensor(
+                gw[:, t, :], got[t][:], twice_rowf[:, t:t + 1], rests[t][:], ALU.mult, ALU.add
+            )
+        for h in range(2):
+            cols = slice(h * HALF, (h + 1) * HALF)
+            nc.scalar.activation(got[last][:, cols], places[last][:].indirect(get_list[:, 16 * h:16 * (h + 1)]), ACT.Copy)
+        for h in range(2):
+            cols = slice(h * HALF, (h + 1) * HALF)
+            nc.vector.scalar_tensor_tensor(
+                gw[:, last, cols], got[last][:, cols], twice_rowf[:, last:last + 1], rests[last][:, cols],
+                ALU.mult, ALU.add,
+            )
+
         woven = keep.tile([P, SLOTS, PACK], BF16, name="woven", align_bytes=64)
         gw_codes = keep.tile([P, SLOTS], U32, name="gw_codes", align_bytes=64)
         gw_scales = keep.tile([P, SLOTS], U8, name="gw_scales", align_bytes=64)
-        got_last = keep.tile([P, HALF], F32, name="got_last")
-        nc.scalar.activation(got_last[:], places[last][:].indirect(get_list[:, 16:32]), ACT.Copy)
-        for h in range(2):
-            cols = slice(h * HALF, (h + 1) * HALF)
-            if h == 0:
-                nc.vector.tensor_tensor(
-                    half_g[last][:, cols], places[last][:].indirect(get_list[:, 0:16]), rests[last][:, cols], ALU.add
-                )
-            else:
-                nc.vector.tensor_tensor(half_g[last][:, cols], got_last[:], rests[last][:, cols], ALU.add)
-            nc.vector.tensor_scalar(gw[:, last, cols], half_g[last][:, cols], twice_rowf[:, last:last + 1], None, ALU.mult)
-            nc.vector.tensor_copy(
+        for n, (first, width) in enumerate(((0, 128), (128, 128), (256, 128), (384, 128))):
+            cols = slice(first, first + width)
+            (nc.vector.tensor_copy if n < 2 else nc.scalar.copy)(
                 out=woven[:, cols, :].rearrange("p (c i) t -> p c t i", i=2),
                 in_=gw[:, :, cols].rearrange("p t (c i) -> p c t i", i=2),
             )
@@ -185,10 +185,10 @@ def tile_attend_openbridge_twoq_mixed_kernel(
                 scales=gw_scales[:, cols],
                 in_=woven[:, cols, :].rearrange("p i t -> p (i t)"),
             )
-            bank = psum.tile([P, BANK], F32, name="bank")
+            bank = psum.tile([P, BANK], F32, name="bank%d" % (4 + n))
             for c in range(2):
                 nc.tensor.matmul_mx(
-                    out=bank[:, c * HALF:(c + 1) * HALF],
+                    out=bank[:, c * width:(c + 1) * width],
                     lhsT=mix_w[:, c * P:(c + 1) * P].bitcast(FP8X4),
                     lhsT_scale=mix_s[:, c * P:(c + 1) * P],
                     rhs=gw_codes[:, cols].bitcast(FP8X4),
@@ -196,6 +196,6 @@ def tile_attend_openbridge_twoq_mixed_kernel(
                     start=True,
                     stop=True,
                 )
-            result = keep.tile([P, 2, HALF], F32, name="result%d" % h)
-            nc.scalar.copy(result[:].rearrange("p c i -> p (c i)"), bank[:])
+            result = keep.tile([P, 2, width], F32, name="result%d" % n)
+            nc.scalar.copy(result[:].rearrange("p c i -> p (c i)"), bank[:, :2 * width])
             nc.sync.dma_start(out=out.rearrange("(c e) i -> e c i", c=2)[:, :, cols], in_=result[:])

from contextlib import ExitStack

import concourse.mybir as mybir

F32 = mybir.dt.float32
BF16 = mybir.dt.bfloat16
I32 = mybir.dt.int32
U32 = mybir.dt.uint32
U16 = mybir.dt.uint16
U8 = mybir.dt.uint8
FP8X4 = mybir.dt.float8_e4m3fn_x4
FP4X4 = mybir.dt.float4_e2m1fn_x4
ALU = mybir.AluOpType
ACT = mybir.ActivationFunctionType

P = 128
PACK = 4
D, T, U, Z, SLOTS, Q, E = 512, 1024, 1024, 1024, 512, 512, 256
BANK = 512
HALF = 256

FLOPS = 2 * D * Q * T + 2 * D * Q * U + 2 * Q * E * SLOTS


def tile_attend_openbridge_twoq_mixed_kernel(
    tc, query, query2, keys_words, keys_scales, notes_words, notes_scales, thr, slope, rowf,
    mix_words, mix_scales, offs, offs2, offs3, offs4, out,
):
    nc = tc.nc
    with ExitStack() as ctx:
        keep = ctx.enter_context(tc.tile_pool(name="keep", bufs=1))
        psum = ctx.enter_context(tc.psum_pool(name="psum", bufs=1))

        def scale_plane(name, source, width, queue):
            plane = keep.tile([P, width], U8, name=name, align_bytes=64)
            for r in range(4):
                queue.dma_start(out=plane[r:P:32, :].bitcast(I32), in_=source[0, r:16:4, :].bitcast(I32))
            return plane

        def load_rows(name, source):
            raw = keep.tile([P, PACK, Q], F32, name=name)
            nc.sync.dma_start(out=raw[:], in_=source.rearrange("(p j) q -> p j q", j=PACK))
            return raw

        def load_list(name, source):
            offsets = keep.tile([P, SLOTS // 16], U16, name=name)
            nc.sync.dma_start(offsets[:], source)
            return offsets

        def load_vector(name, source, queue):
            vec = keep.tile([P, PACK], F32, name=name)
            queue.dma_start(out=vec[:], in_=source.rearrange("(p t) o -> p (t o)", t=PACK))
            return vec

        def load_words(name, source, cols):
            words = keep.tile([P, cols.stop - cols.start], U32, name=name, align_bytes=64)
            nc.sync.dma_start(
                out=words[:].bitcast(I32), in_=source[0].rearrange("p n t -> p (n t)").bitcast(I32)[:, cols]
            )
            return words

        q_raw = load_rows("q_raw", query)
        key_scales = scale_plane("key_scales", keys_scales, T, nc.sync)
        key_words = keep.tile([P, 2 * T], U8, name="key_words", align_bytes=64)
        nc.sync.dma_start(out=key_words[:].bitcast(I32), in_=keys_words[0].bitcast(I32))
        a_list = load_list("a_list", offs)
        slope_t = load_vector("slope_t", slope, nc.gpsimd)
        thr_t = load_vector("thr_t", thr, nc.gpsimd)
        q2_raw = load_rows("q2_raw", query2)
        note_words = load_words("note_words", notes_words, slice(0, U))
        note_scales = scale_plane("note_scales", notes_scales, U, nc.sync)
        b_list = load_list("b_list", offs2)
        put_list = load_list("put_list", offs3)
        rowf_t = load_vector("rowf_t", rowf, nc.sync)
        get_list = load_list("get_list", offs4)
        mix_w = load_words("mix_w", mix_words, slice(0, E))
        mix_s = scale_plane("mix_s", mix_scales, E, nc.sync)

        places = [keep.tile([P, Z], F32, name="places%d" % t) for t in range(PACK)]
        for tile in places:
            nc.vector.memset(tile[:], 0.0)

        def quantise_queries(name, raw, staging):
            codes = keep.tile([P, Q], U32, name=name + "_codes", align_bytes=64)
            scales = keep.tile([P, Q], U8, name=name + "_scales", align_bytes=64)
            for pair in range(2):
                ts = slice(2 * pair, 2 * pair + 2)
                dealt = keep.tile([P, 2, P, PACK], BF16, name=staging[pair], align_bytes=64)
                nc.vector.tensor_copy(
                    out=dealt[:].rearrange("p t m j -> p m j t"),
                    in_=raw[:].rearrange("p j (m t) -> p m j t", t=PACK)[:, :, :, ts],
                )
                for t in range(2 * pair, 2 * pair + 2):
                    nc.vector.quantize_mx(
                        out=codes[:, t * P:(t + 1) * P].bitcast(FP8X4),
                        scales=scales[:, t * P:(t + 1) * P],
                        in_=dealt[:, t % 2].rearrange("p m j -> p (m j)"),
                    )
            return codes, scales

        q_codes, q_scales = quantise_queries("q", q_raw, ("q_dealt", "q_dealt"))
        q2_codes, q2_scales = quantise_queries("q2", q2_raw, ("q2_dealt0", "q2_dealt1"))

        twice_rowf = keep.tile([P, PACK], F32, name="twice_rowf")
        nc.vector.tensor_scalar(twice_rowf[:], rowf_t[:], 2.0, None, ALU.mult)

        gw = keep.tile([P, PACK, SLOTS], F32, name="gw")

        def scores(name, t, codes, scales, moving, moving_scales, copy_engines, pair):
            rows = keep.tile([P, 2 * BANK], F32, name="%s%d" % (name, t))
            for h in range(2):
                bank = psum.tile([P, BANK], F32, name="bank%d" % (2 * pair + h))
                nc.tensor.matmul_mx(
                    out=bank[:],
                    lhsT=codes[:, t * P:(t + 1) * P].bitcast(FP8X4),
                    lhsT_scale=scales[:, t * P:(t + 1) * P],
                    rhs=moving[h],
                    rhs_scale=moving_scales[:, h * BANK:(h + 1) * BANK],
                    start=True,
                    stop=True,
                )
                copy_engines[h](rows[:, h * BANK:(h + 1) * BANK], bank[:])
            return rows

        keys_moving = [key_words[:, h * 2 * BANK:(h + 1) * 2 * BANK].bitcast(FP4X4) for h in range(2)]
        notes_moving = [note_words[:, h * BANK:(h + 1) * BANK].bitcast(FP8X4) for h in range(2)]
        on_scalar = (nc.scalar.copy, nc.scalar.copy)
        shared = (nc.scalar.copy, nc.vector.tensor_copy)

        on_vector = (nc.vector.tensor_copy, nc.vector.tensor_copy)
        rests = []
        for t in range(PACK):
            a = scores("a", t, q_codes, q_scales, keys_moving, key_scales, on_scalar, t)
            gate = keep.tile([P, SLOTS], F32, name="gate%d" % t)
            nc.scalar.activation(
                gate[:], a[:].indirect(a_list[:]), ACT.Sigmoid, bias=thr_t[:, t:t + 1], scale=slope_t[:, t:t + 1]
            )
            b = scores("b", t, q2_codes, q2_scales, notes_moving, note_scales,
                       on_vector if t == 0 else on_scalar, (t + 2) % 4)
            note = keep.tile([P, SLOTS], F32, name="note%d" % t)
            if t == 0:
                nc.vector.tensor_copy(note[:], b[:].indirect(b_list[:]))
            else:
                nc.scalar.activation(note[:], b[:].indirect(b_list[:]), ACT.Copy)
            nc.vector.tensor_tensor(places[t][:].indirect(put_list[:]), note[:], gate[:], ALU.mult)
            scaled_gate = keep.tile([P, SLOTS], F32, name="scaled_gate%d" % t)
            if t < 2:
                nc.vector.tensor_scalar(scaled_gate[:], gate[:], twice_rowf[:, t:t + 1], None, ALU.mult)
            else:
                nc.scalar.activation(scaled_gate[:], gate[:], ACT.Copy, scale=twice_rowf[:, t:t + 1])
            rest = keep.tile([P, SLOTS], F32, name="rest%d" % t)
            nc.vector.scalar_tensor_tensor(
                rest[:], note[:], rowf_t[:, t:t + 1], scaled_gate[:], ALU.mult, ALU.subtract
            )
            rests.append(rest)

        last = PACK - 1
        got = [keep.tile([P, SLOTS], F32, name="got%d" % t) for t in range(PACK)]
        for t in range(last):
            nc.scalar.activation(got[t][:], places[t][:].indirect(get_list[:]), ACT.Copy)
            nc.vector.scalar_tensor_tensor(
                gw[:, t, :], got[t][:], twice_rowf[:, t:t + 1], rests[t][:], ALU.mult, ALU.add
            )
        for h in range(2):
            cols = slice(h * HALF, (h + 1) * HALF)
            nc.scalar.activation(got[last][:, cols], places[last][:].indirect(get_list[:, 16 * h:16 * (h + 1)]), ACT.Copy)
        for h in range(2):
            cols = slice(h * HALF, (h + 1) * HALF)
            nc.vector.scalar_tensor_tensor(
                gw[:, last, cols], got[last][:, cols], twice_rowf[:, last:last + 1], rests[last][:, cols],
                ALU.mult, ALU.add,
            )

        woven = keep.tile([P, SLOTS, PACK], BF16, name="woven", align_bytes=64)
        gw_codes = keep.tile([P, SLOTS], U32, name="gw_codes", align_bytes=64)
        gw_scales = keep.tile([P, SLOTS], U8, name="gw_scales", align_bytes=64)
        for n, (first, width) in enumerate(((0, 128), (128, 128), (256, 128), (384, 128))):
            cols = slice(first, first + width)
            (nc.vector.tensor_copy if n < 2 else nc.scalar.copy)(
                out=woven[:, cols, :].rearrange("p (c i) t -> p c t i", i=2),
                in_=gw[:, :, cols].rearrange("p t (c i) -> p c t i", i=2),
            )
            nc.vector.quantize_mx(
                out=gw_codes[:, cols].bitcast(FP8X4),
                scales=gw_scales[:, cols],
                in_=woven[:, cols, :].rearrange("p i t -> p (i t)"),
            )
            bank = psum.tile([P, BANK], F32, name="bank%d" % (4 + n))
            for c in range(2):
                nc.tensor.matmul_mx(
                    out=bank[:, c * width:(c + 1) * width],
                    lhsT=mix_w[:, c * P:(c + 1) * P].bitcast(FP8X4),
                    lhsT_scale=mix_s[:, c * P:(c + 1) * P],
                    rhs=gw_codes[:, cols].bitcast(FP8X4),
                    rhs_scale=gw_scales[:, cols],
                    start=True,
                    stop=True,
                )
            result = keep.tile([P, 2, width], F32, name="result%d" % n)
            nc.scalar.copy(result[:].rearrange("p c i -> p (c i)"), bank[:, :2 * width])
            nc.sync.dma_start(out=out.rearrange("(c e) i -> e c i", c=2)[:, :, cols], in_=result[:])
